import numpy as np
import ml_dtypes


def mxq(x, axis, fmt="e4m3"):
    dtype, down = {"e4m3": (ml_dtypes.float8_e4m3fn, 7), "e5m2": (ml_dtypes.float8_e5m2, 14)}[fmt]
    v = np.moveaxis(np.asarray(x, np.float32).astype(ml_dtypes.bfloat16).astype(np.float64), axis, -1)
    blocks = v.reshape(v.shape[:-1] + (-1, 32))
    amax = np.abs(blocks).max(-1, keepdims=True)
    byte = np.maximum(np.where(amax > 0, np.frexp(amax)[1] - 1 + 127, 0) - down, 1)
    scale = np.exp2(byte - 127.0)
    codes = (blocks / scale).astype(np.float32).astype(dtype).astype(np.float64)
    return np.moveaxis((codes * scale).reshape(v.shape), -1, axis)


WIDE = False


def mx_kscale(k):
    if not WIDE:
        return np.ones(k)
    levels = np.array([10, -10, 5, -5, 0])
    if k % 512:
        return np.exp2(np.random.permutation(np.resize(levels, k // 32))).repeat(32)
    a = np.empty((k // 512, 16))
    for p in range(k // 512):
        a[p, :8] = np.random.permutation(np.resize(levels, 8))
        for g in range(8):
            far = levels[np.abs(levels - a[p, g]) >= 10]
            a[p, g + 8] = far[np.random.randint(len(far))]
    return np.exp2(a.ravel()).repeat(32)


def f64(x):
    return np.asarray(x).astype(np.float64)


def striped(idx):
    return np.tile(idx.reshape(-1, 16).T, (8, 1)).astype(np.uint16)


def unstriped(offs):
    return offs[:16].T.reshape(-1).astype(np.int64)


def striped8(idx):
    return np.concatenate([x.reshape(-1, 16).T for x in idx]).astype(np.uint16)


def runs(offs, k):
    lists = np.stack([offs[16 * r : 16 * r + 16].T.reshape(-1) for r in range(8)]).astype(np.int64)
    return lists[np.arange(k) % 512 // 64]


def pack_weight(w):
    k, n = w.shape
    w = f64(np.asarray(w, np.float32).astype(ml_dtypes.bfloat16)).reshape(k // 32, 32, n)
    amax = np.abs(w).max(1)
    byte = np.clip(np.where(amax > 0, np.frexp(amax)[1] - 1 + 127 - 7, 1), 1, 254)
    scaled = (w * np.exp2(127.0 - byte)[:, None, :]).reshape(k, n).astype(np.float32)
    words = np.ascontiguousarray(scaled.reshape(k // 512, 128, 4, n).transpose(0, 1, 3, 2)).astype(ml_dtypes.float8_e4m3fn).view(np.uint8)
    return words, np.ascontiguousarray(byte.astype(np.uint8).reshape(k // 512, 16, n))


def unpack_weight(words, scales):
    g, p, n, _ = words.shape
    vals = np.ascontiguousarray(words).view(ml_dtypes.float8_e4m3fn).astype(np.float64) * np.repeat(np.exp2(scales.astype(np.float64) - 127.0), 8, axis=1)[..., None]
    return vals.transpose(0, 1, 3, 2).reshape(g * 512, n)


K, T, S, H, C = 512, 2048, 512, 512, 512


def setup_inputs():
    n = np.random.standard_normal
    s = mx_kscale(K)[:, None]
    packed_xT = pack_weight(n((K, T)) * s)
    return {
        "x_words": packed_xT[0],
        "x_scales": packed_xT[1],
        "w1": (n((K, H)) / np.sqrt(K) / s).astype(np.float32),
        "w2": (n((K, H)) / np.sqrt(K) / s).astype(np.float32),
        "gs": (np.random.uniform(0.5, 1.5, (K, 1)) / s).astype(np.float32),
        "offs": striped(np.random.permutation(T)[:S]),
        "two": striped(np.random.permutation(T)[:S]),
        "lf": striped8(np.stack([np.random.permutation(S) for _ in range(8)])),
        "rt": striped8(np.stack([np.random.permutation(S) for _ in range(8)])),
        "cand": striped(np.random.permutation(T)[:C]),
    }


def reference(x_words, x_scales, w1, w2, gs, offs, two, lf, rt, cand):
    x_cand = unpack_weight(x_words, x_scales)[:, unstriped(cand)]
    x_two = unpack_weight(x_words, x_scales)[:, unstriped(two)]
    c = mxq(f64(w2), 0, "e4m3").T @ x_two
    xq = unpack_weight(x_words, x_scales)[:, unstriped(offs)]
    y = mxq(f64(w1), 0, "e4m3").T @ xq
    e2 = y + 0.5 * (c - (c[np.arange(H)[:, None], runs(lf, H)]))
    z = f64(gs) * (c + 0.5 * (e2[np.arange(H)[:, None], runs(rt, H)] - e2))
    return 0.0625 * ((x_cand.T @ mxq(z, 0, "e4m3")))

@@ -1,0 +1,199 @@
+from contextlib import ExitStack
+
+import concourse.mybir as mybir
+
+K, T, S, H, C = 512, 2048, 512, 512, 512
+FLOPS = 3 * 2 * K * H * S
+
+F32 = mybir.dt.float32
+BF16 = mybir.dt.bfloat16
+I32 = mybir.dt.int32
+U32 = mybir.dt.uint32
+U16 = mybir.dt.uint16
+U8 = mybir.dt.uint8
+FP8X4 = mybir.dt.float8_e4m3fn_x4
+ALU = mybir.AluOpType
+COPY = mybir.ActivationFunctionType.Copy
+
+P = 128
+PACK = 4
+LANES = 16
+HALF = S // 2
+W1_CHUNKS = ((0, 64), (64, 128))
+PLACE_CHUNKS = ((0, 256), (256, 384), (384, 512))
+SUMMED_PLANES = 3
+
+
+def tile_picked_fdtd8_none_p_kernel(tc, x_words, x_scales, w1, w2, gs, offs, two, lf, rt, cand, out):
+    nc = tc.nc
+    with ExitStack() as ctx:
+        keep = ctx.enter_context(tc.tile_pool(name="keep", bufs=1))
+        psum = ctx.enter_context(tc.psum_pool(name="psum", bufs=1))
+
+        def load_list(name, src):
+            tile = keep.tile([P, S // LANES], U16, name=name)
+            nc.sync.dma_start(tile[:], src)
+            return tile
+
+        def entries(tile, a, b):
+            return tile[:, a // LANES : b // LANES]
+
+        def bank(n, shape):
+            return psum.tile(shape, F32, name="bank%d" % n, tag="bank%d" % n)
+
+        table_scales = keep.tile([P, T], U8, name="table_scales", align_bytes=64)
+        nc.vector.memset(table_scales[:].bitcast(I32), 0)
+        for q in range(4):
+            nc.scalar.dma_start(table_scales[32 * q : 32 * q + 4, :].bitcast(I32), x_scales[0][4 * q : 4 * q + 4, :].bitcast(I32))
+        gain = keep.tile([P, PACK], F32, name="gain")
+        nc.gpsimd.dma_start(gain[:], gs.rearrange("(p t) o -> p (t o)", t=PACK))
+
+        two_list = load_list("two_list", two)
+        offs_list = load_list("offs_list", offs)
+        cand_list = load_list("cand_list", cand)
+        w2_raw = keep.tile([P, PACK, H], F32, name="w2_raw")
+        nc.sync.dma_start(w2_raw[:], w2.rearrange("(p j) c -> p j c", j=PACK))
+        table_words = keep.tile([P, T], U32, name="table_words", align_bytes=64)
+        nc.sync.dma_start(table_words[:].bitcast(I32), x_words[0].rearrange("p n t -> p (n t)").bitcast(I32))
+        w1_raw = []
+        for m0, m1 in W1_CHUNKS:
+            part = keep.tile([P, PACK, PACK * (m1 - m0)], F32, name="w1_raw%d" % m0)
+            nc.sync.dma_start(part[:], w1.rearrange("(p j) c -> p j c", j=PACK)[:, :, PACK * m0 : PACK * m1])
+            w1_raw.append(part)
+        lf_list = load_list("lf_list", lf)
+        rt_list = load_list("rt_list", rt)
+
+        factor = keep.tile([P, PACK], F32, name="factor")
+        nc.scalar.activation(factor[:], gain[:], COPY, scale=-0.25)
+
+        def pick(name, table, dtype, lst):
+            tile = keep.tile([P, S], dtype, name=name, align_bytes=64)
+            nc.vector.tensor_copy(tile[:], table[:].indirect(lst[:]))
+            return tile
+
+        def deal(grouped, raw, m0, m1, scale):
+            nc.scalar.activation(
+                grouped[:].rearrange("p (t m j) -> p m j t", t=PACK, j=PACK)[:, m0:m1, :, :],
+                raw[:].rearrange("p j (m t) -> p m j t", t=PACK),
+                COPY,
+                scale=scale,
+            )
+
+        def quantise(name, grouped, width):
+            codes = keep.tile([P, width], U32, name=name + "_codes", align_bytes=64)
+            scales = keep.tile([P, width], U8, name=name + "_scales", align_bytes=64)
+            nc.vector.quantize_mx(out=codes[:].bitcast(FP8X4), scales=scales[:], in_=grouped[:])
+            return codes, scales
+
+        def product(dst, stationary, cols, moving, start, stop):
+            nc.tensor.matmul_mx(
+                out=dst,
+                lhsT=stationary[0][:, cols].bitcast(FP8X4),
+                lhsT_scale=stationary[1][:, cols],
+                rhs=moving[0][:].bitcast(FP8X4),
+                rhs_scale=moving[1][:],
+                start=start,
+                stop=stop,
+            )
+
+        two_scales = pick("two_scales", table_scales, U8, two_list)
+        offs_scales = pick("offs_scales", table_scales, U8, offs_list)
+        cand_scales = pick("cand_scales", table_scales, U8, cand_list)
+
+        w2_grouped = keep.tile([P, PACK * H], BF16, name="w2_grouped", align_bytes=64)
+        deal(w2_grouped, w2_raw, 0, P, 1.0)
+        w1_grouped = keep.tile([P, PACK * H], BF16, name="w1_grouped", align_bytes=64)
+        for (m0, m1), part in zip(W1_CHUNKS, w1_raw):
+            deal(w1_grouped, part, m0, m1, 2.0)
+
+        x_two = (pick("two_words", table_words, U32, two_list), two_scales)
+        w2_mx = quantise("w2", w2_grouped, H)
+        x_offs = (pick("offs_words", table_words, U32, offs_list), offs_scales)
+        w1_mx = quantise("w1", w1_grouped, H)
+        x_cand = (pick("cand_words", table_words, U32, cand_list), cand_scales)
+
+        planes = [slice(P * t, P * (t + 1)) for t in range(PACK)]
+        c_scaled = []
+        for t in range(PACK):
+            c_bank = bank(t, [P, S])
+            product(c_bank[:], w2_mx, planes[t], x_two, True, True)
+            tile = keep.tile([P, S], F32, name="c_scaled%d" % t)
+            nc.scalar.activation(tile[:], c_bank[:], COPY, scale=factor[:, t : t + 1])
+            c_scaled.append(tile)
+
+        local = []
+        for t in range(PACK):
+            y_bank = bank(PACK + t, [P, S])
+            tile = keep.tile([P, S], F32, name="local%d" % t)
+            if t < SUMMED_PLANES:
+                product(y_bank[:], w2_mx, planes[t], x_two, True, False)
+                product(y_bank[:], w1_mx, planes[t], x_offs, False, True)
+                nc.scalar.activation(tile[:], y_bank[:], COPY, scale=factor[:, t : t + 1])
+            else:
+                product(y_bank[:], w1_mx, planes[t], x_offs, True, True)
+                nc.vector.scalar_tensor_tensor(tile[:], y_bank[:], factor[:, t : t + 1], c_scaled[t][:], ALU.mult, ALU.add)
+            local.append(tile)
+
+        e_scaled = [keep.tile([P, S], F32, name="e_scaled%d" % t) for t in range(PACK)]
+        rest = [keep.tile([P, S], F32, name="rest%d" % t) for t in range(PACK)]
+
+        def left(t):
+            for a in (0, HALF):
+                nc.vector.tensor_tensor(
+                    e_scaled[t][:, a : a + HALF],
+                    c_scaled[t][:].indirect(entries(lf_list, a, a + HALF)),
+                    local[t][:, a : a + HALF],
+                    ALU.subtract,
+                )
+
+        def remainder(t):
+            nc.vector.scalar_tensor_tensor(rest[t][:], c_scaled[t][:], 4.0, e_scaled[t][:], ALU.mult, ALU.add)
+
+        left(0)
+        for t in range(1, PACK):
+            left(t)
+            remainder(t - 1)
+        remainder(PACK - 1)
+
+        out_view = out.rearrange("(a p) j -> p a j", p=P)
+        z_grouped = {}
+
+        def right(n):
+            a, b = PLACE_CHUNKS[n]
+            z_planes = keep.tile([P, PACK, b - a], F32, name="z_planes%d" % n)
+            for t in range(PACK):
+                nc.vector.tensor_tensor(z_planes[:, t, :], e_scaled[t][:].indirect(entries(rt_list, a, b)), rest[t][:, a:b], ALU.subtract)
+            grouped = keep.tile([P, PACK * (b - a)], BF16, name="z_grouped%d" % n, align_bytes=64)
+            dst = grouped[:].rearrange("p (c i t) -> p c t i", i=4, t=PACK)
+            src = z_planes[:].rearrange("p t (c i) -> p c t i", i=4)
+            if n == len(PLACE_CHUNKS) - 1:
+                nc.vector.tensor_copy(dst, src)
+            else:
+                nc.scalar.copy(dst, src)
+            z_grouped[n] = grouped
+
+        def score(n):
+            a, b = PLACE_CHUNKS[n]
+            width = b - a
+            last = n == len(PLACE_CHUNKS) - 1
+            z_mx = quantise("z%d" % n, z_grouped[n], width)
+            for h in range(2):
+                acc = bank(2 * n + h, [P, 2, width])
+                for u in range(2):
+                    product(acc[:, u, :], x_cand, planes[2 * h + u], z_mx, True, True)
+                result = keep.tile([P, 2, width], F32, name="result%d_%d" % (n, h))
+                if last and h == 1:
+                    nc.vector.tensor_scalar(result[:], acc[:], 0.0625, None, ALU.mult)
+                    nc.sync.dma_start(out_view[:, 2 * h : 2 * h + 2, a:b], result[:])
+                elif last:
+                    nc.scalar.activation(result[:], acc[:], COPY, scale=0.0625)
+                    nc.scalar.dma_start(out_view[:, 2 * h : 2 * h + 2, a:b], result[:])
+                else:
+                    nc.scalar.activation(result[:], acc[:], COPY, scale=0.0625)
+                    nc.sync.dma_start(out_view[:, 2 * h : 2 * h + 2, a:b], result[:])
+
+        right(0)
+        for n in range(1, len(PLACE_CHUNKS)):
+            right(n)
+            score(n - 1)
+        score(len(PLACE_CHUNKS) - 1)

@@ -1,6 +1,7 @@
 from contextlib import ExitStack
 
 import concourse.mybir as mybir
+from concourse.masks import make_identity
 
 K, T, S, H, C = 512, 2048, 512, 512, 512
 FLOPS = 3 * 2 * K * H * S
@@ -19,8 +20,9 @@ P = 128
 PACK = 4
 LANES = 16
 HALF = S // 2
-W1_CHUNKS = ((0, 64), (64, 128))
-PLACE_CHUNKS = ((0, 256), (256, 384), (384, 512))
+W_CHUNKS = ((0, 64), (64, 128))
+CHUNKS = S // P
+TURNED = 3
 SUMMED_PLANES = 3
 
 
@@ -43,31 +45,33 @@ def tile_picked_fdtd8_none_p_kernel(tc, x_words, x_scales, w1, w2, gs, offs, two
 
         table_scales = keep.tile([P, T], U8, name="table_scales", align_bytes=64)
         nc.vector.memset(table_scales[:].bitcast(I32), 0)
-        for q in range(4):
-            nc.scalar.dma_start(table_scales[32 * q : 32 * q + 4, :].bitcast(I32), x_scales[0][4 * q : 4 * q + 4, :].bitcast(I32))
-        gain = keep.tile([P, PACK], F32, name="gain")
-        nc.gpsimd.dma_start(gain[:], gs.rearrange("(p t) o -> p (t o)", t=PACK))
-
+        identity = keep.tile([P, P], F32, name="identity")
+        make_identity(nc, identity[:])
         two_list = load_list("two_list", two)
         offs_list = load_list("offs_list", offs)
         cand_list = load_list("cand_list", cand)
-        w2_raw = keep.tile([P, PACK, H], F32, name="w2_raw")
-        nc.sync.dma_start(w2_raw[:], w2.rearrange("(p j) c -> p j c", j=PACK))
+        for q in range(4):
+            nc.sync.dma_start(table_scales[32 * q : 32 * q + 4, :].bitcast(I32), x_scales[0][4 * q : 4 * q + 4, :].bitcast(I32))
         table_words = keep.tile([P, T], U32, name="table_words", align_bytes=64)
         nc.sync.dma_start(table_words[:].bitcast(I32), x_words[0].rearrange("p n t -> p (n t)").bitcast(I32))
-        w1_raw = []
-        for m0, m1 in W1_CHUNKS:
-            part = keep.tile([P, PACK, PACK * (m1 - m0)], F32, name="w1_raw%d" % m0)
-            nc.sync.dma_start(part[:], w1.rearrange("(p j) c -> p j c", j=PACK)[:, :, PACK * m0 : PACK * m1])
-            w1_raw.append(part)
+
+        def load_weight(name, w):
+            parts = []
+            for m0, m1 in W_CHUNKS:
+                part = keep.tile([P, PACK, PACK * (m1 - m0)], F32, name="%s_raw%d" % (name, m0), tag="%s_raw%d" % (name, m0))
+                nc.sync.dma_start(part[:], w.rearrange("(p j) c -> p j c", j=PACK)[:, :, PACK * m0 : PACK * m1])
+                parts.append(part)
+            return parts
+
+        w2_raw = load_weight("w2", w2)
+        gain = keep.tile([P, PACK], F32, name="gain")
+        nc.sync.dma_start(gain[:], gs.rearrange("(p t) o -> p (t o)", t=PACK))
+        w1_raw = load_weight("w1", w1)
         lf_list = load_list("lf_list", lf)
         rt_list = load_list("rt_list", rt)
 
-        factor = keep.tile([P, PACK], F32, name="factor")
-        nc.scalar.activation(factor[:], gain[:], COPY, scale=-0.25)
-
-        def pick(name, table, dtype, lst):
-            tile = keep.tile([P, S], dtype, name=name, align_bytes=64)
+        def pick(name, table, dtype, lst, tag=None):
+            tile = keep.tile([P, S], dtype, name=name, tag=tag or name, align_bytes=64)
             nc.vector.tensor_copy(tile[:], table[:].indirect(lst[:]))
             return tile
 
@@ -100,100 +104,139 @@ def tile_picked_fdtd8_none_p_kernel(tc, x_words, x_scales, w1, w2, gs, offs, two
         offs_scales = pick("offs_scales", table_scales, U8, offs_list)
         cand_scales = pick("cand_scales", table_scales, U8, cand_list)
 
-        w2_grouped = keep.tile([P, PACK * H], BF16, name="w2_grouped", align_bytes=64)
-        deal(w2_grouped, w2_raw, 0, P, 1.0)
-        w1_grouped = keep.tile([P, PACK * H], BF16, name="w1_grouped", align_bytes=64)
-        for (m0, m1), part in zip(W1_CHUNKS, w1_raw):
+        w2_grouped = keep.tile([P, PACK * H], BF16, name="w2_grouped", tag="w2_grouped", align_bytes=64)
+        for (m0, m1), part in zip(W_CHUNKS, w2_raw):
+            deal(w2_grouped, part, m0, m1, 1.0)
+        w1_grouped = keep.tile([P, PACK * H], BF16, name="w1_grouped", tag="w1_grouped", align_bytes=64)
+        for (m0, m1), part in zip(W_CHUNKS, w1_raw):
             deal(w1_grouped, part, m0, m1, 2.0)
+        factors = keep.tile([P, 3 * PACK], F32, name="factors", tag="w1_raw%d" % W_CHUNKS[-1][0])
+        factor, factor4, opposite = factors[:, :PACK], factors[:, PACK : 2 * PACK], factors[:, 2 * PACK :]
+        nc.scalar.activation(factor, gain[:], COPY, scale=-0.25)
 
         x_two = (pick("two_words", table_words, U32, two_list), two_scales)
-        w2_mx = quantise("w2", w2_grouped, H)
         x_offs = (pick("offs_words", table_words, U32, offs_list), offs_scales)
+        w2_mx = quantise("w2", w2_grouped, H)
+        x_cand = (pick("cand_words", table_words, U32, cand_list, "w2_grouped"), cand_scales)
         w1_mx = quantise("w1", w1_grouped, H)
-        x_cand = (pick("cand_words", table_words, U32, cand_list), cand_scales)
 
         planes = [slice(P * t, P * (t + 1)) for t in range(PACK)]
-        c_scaled = []
+        c_banks = [bank(t, [P, S]) for t in range(PACK)]
+        y_banks = [bank(PACK + t, [P, S]) for t in range(PACK)]
+        c_scaled = [keep.tile([P, S], F32, name="c_scaled%d" % t) for t in range(PACK)]
+        local = [keep.tile([P, S], F32, name="local%d" % t) for t in range(PACK)]
         for t in range(PACK):
-            c_bank = bank(t, [P, S])
-            product(c_bank[:], w2_mx, planes[t], x_two, True, True)
-            tile = keep.tile([P, S], F32, name="c_scaled%d" % t)
-            nc.scalar.activation(tile[:], c_bank[:], COPY, scale=factor[:, t : t + 1])
-            c_scaled.append(tile)
+            product(c_banks[t][:], w2_mx, planes[t], x_two, True, True)
+            nc.scalar.activation(c_scaled[t][:], c_banks[t][:], COPY, scale=factor[:, t : t + 1])
+            passes = [(w2_mx, x_two), (w1_mx, x_offs)]
+            if t == 2:
+                passes = passes[::-1]
+            if t == 3:
+                passes = passes[1:]
+            for u, (stationary, moving) in enumerate(passes):
+                product(y_banks[t][:], stationary, planes[t], moving, u == 0, u == len(passes) - 1)
+            if t == 0:
+                nc.scalar.activation(opposite, gain[:], COPY, scale=0.25)
+            elif t < SUMMED_PLANES:
+                nc.scalar.activation(local[t][:], y_banks[t][:], COPY, scale=factor[:, t : t + 1])
+        nc.scalar.activation(factor4, gain[:], COPY, scale=-1.0)
 
-        local = []
+        turned = TURNED * P
+        c_full = []
         for t in range(PACK):
-            y_bank = bank(PACK + t, [P, S])
-            tile = keep.tile([P, S], F32, name="local%d" % t)
-            if t < SUMMED_PLANES:
-                product(y_bank[:], w2_mx, planes[t], x_two, True, False)
-                product(y_bank[:], w1_mx, planes[t], x_offs, False, True)
-                nc.scalar.activation(tile[:], y_bank[:], COPY, scale=factor[:, t : t + 1])
-            else:
-                product(y_bank[:], w1_mx, planes[t], x_offs, True, True)
-                nc.vector.scalar_tensor_tensor(tile[:], y_bank[:], factor[:, t : t + 1], c_scaled[t][:], ALU.mult, ALU.add)
-            local.append(tile)
+            tile = keep.tile([P, turned], F32, name="c_full%d" % t)
+            nc.scalar.activation(tile[:], c_banks[t][:, :turned], COPY, scale=factor4[:, t : t + 1])
+            c_full.append(tile)
+
+        sums = [bank(PACK + n, [P, PACK, P]) for n in range(TURNED)]
+
+        def add_turned(n, t, src, start, stop):
+            nc.tensor.matmul(sums[n][:, t, :], src, identity[:], start=start, stop=stop, is_transpose=True)
 
         e_scaled = [keep.tile([P, S], F32, name="e_scaled%d" % t) for t in range(PACK)]
-        rest = [keep.tile([P, S], F32, name="rest%d" % t) for t in range(PACK)]
-
-        def left(t):
+        for t in range(PACK):
+            if t == SUMMED_PLANES - 1:
+                nc.vector.scalar_tensor_tensor(local[t + 1][:], y_banks[t + 1][:], factor[:, t + 1 : t + 2], c_scaled[t + 1][:], ALU.mult, ALU.add)
             for a in (0, HALF):
-                nc.vector.tensor_tensor(
-                    e_scaled[t][:, a : a + HALF],
-                    c_scaled[t][:].indirect(entries(lf_list, a, a + HALF)),
-                    local[t][:, a : a + HALF],
-                    ALU.subtract,
-                )
-
-        def remainder(t):
-            nc.vector.scalar_tensor_tensor(rest[t][:], c_scaled[t][:], 4.0, e_scaled[t][:], ALU.mult, ALU.add)
-
-        left(0)
-        for t in range(1, PACK):
-            left(t)
-            remainder(t - 1)
-        remainder(PACK - 1)
+                window = c_scaled[t][:].indirect(entries(lf_list, a, a + HALF))
+                if t == 0:
+                    nc.vector.tensor_copy(local[t][:, a : a + HALF], window)
+                else:
+                    nc.vector.tensor_tensor(e_scaled[t][:, a : a + HALF], window, local[t][:, a : a + HALF], ALU.subtract)
+            if t == 0:
+                nc.vector.scalar_tensor_tensor(e_scaled[t][:], y_banks[t][:], opposite[:, t : t + 1], local[t][:], ALU.mult, ALU.add)
+            for n in range(TURNED):
+                add_turned(n, t, c_full[t][:, planes[n]], t == 0, False)
+                add_turned(n, t, e_scaled[t][:, planes[n]], False, False)
 
         out_view = out.rearrange("(a p) j -> p a j", p=P)
-        z_grouped = {}
+        last = CHUNKS - 1
 
-        def right(n):
-            a, b = PLACE_CHUNKS[n]
-            z_planes = keep.tile([P, PACK, b - a], F32, name="z_planes%d" % n)
+        def shared(name, tag, shape, dtype):
+            return keep.tile(shape, dtype, name=name, tag=tag, align_bytes=64)
+
+        z_last = shared("z_last", "z_last", [P, PACK * P], F32)
+        z_words = [z_last[:, 0:256], z_last[:, 256:512], shared("z_words2", "z_words2", [P, 2 * P], F32)[:]]
+
+        def right_turned(n, tag, back_bank):
+            fetched = shared("fetched%d" % n, tag, [P, PACK, P], F32)
             for t in range(PACK):
-                nc.vector.tensor_tensor(z_planes[:, t, :], e_scaled[t][:].indirect(entries(rt_list, a, b)), rest[t][:, a:b], ALU.subtract)
-            grouped = keep.tile([P, PACK * (b - a)], BF16, name="z_grouped%d" % n, align_bytes=64)
-            dst = grouped[:].rearrange("p (c i t) -> p c t i", i=4, t=PACK)
-            src = z_planes[:].rearrange("p t (c i) -> p c t i", i=4)
-            if n == len(PLACE_CHUNKS) - 1:
-                nc.vector.tensor_copy(dst, src)
-            else:
-                nc.scalar.copy(dst, src)
-            z_grouped[n] = grouped
+                nc.vector.tensor_scalar(fetched[:, t, :], e_scaled[t][:].indirect(entries(rt_list, P * n, P * (n + 1))), -1.0, 0.0, ALU.mult, ALU.add)
+                add_turned(n, t, fetched[:, t, :], False, t == PACK - 1)
+            rounded = shared("rounded%d" % n, "rounded%d" % n, [P, PACK * P], BF16)
+            nc.scalar.activation(
+                rounded[:].rearrange("p (u m e) -> p u m e", u=2, e=2),
+                sums[n][:].rearrange("p (u e) m -> p u m e", e=2),
+                COPY,
+                scale=-1.0,
+            )
+            back = bank(back_bank, [P, 2, P])
+            for u in range(2):
+                nc.tensor.transpose(back[:, u, :], rounded[:].bitcast(F32)[:, planes[u]], identity[:])
+            nc.scalar.copy(z_words[n].rearrange("p (j u) -> p j u", u=2), back[:].rearrange("p u j -> p j u"))
 
-        def score(n):
-            a, b = PLACE_CHUNKS[n]
-            width = b - a
-            last = n == len(PLACE_CHUNKS) - 1
-            z_mx = quantise("z%d" % n, z_grouped[n], width)
-            for h in range(2):
-                acc = bank(2 * n + h, [P, 2, width])
-                for u in range(2):
-                    product(acc[:, u, :], x_cand, planes[2 * h + u], z_mx, True, True)
-                result = keep.tile([P, 2, width], F32, name="result%d_%d" % (n, h))
-                if last and h == 1:
-                    nc.vector.tensor_scalar(result[:], acc[:], 0.0625, None, ALU.mult)
-                    nc.sync.dma_start(out_view[:, 2 * h : 2 * h + 2, a:b], result[:])
-                elif last:
-                    nc.scalar.activation(result[:], acc[:], COPY, scale=0.0625)
-                    nc.scalar.dma_start(out_view[:, 2 * h : 2 * h + 2, a:b], result[:])
-                else:
-                    nc.scalar.activation(result[:], acc[:], COPY, scale=0.0625)
-                    nc.sync.dma_start(out_view[:, 2 * h : 2 * h + 2, a:b], result[:])
+        def quantise_z(n, grouped, tag):
+            codes = shared("z_codes%d" % n, tag, [P, P], U32)
+            scales = shared("z_scales%d" % n, "z_scales%d" % n, [P, P], U8)
+            nc.vector.quantize_mx(out=codes[:].bitcast(FP8X4), scales=scales[:], in_=grouped)
+            return codes, scales
 
-        right(0)
-        for n in range(1, len(PLACE_CHUNKS)):
-            right(n)
-            score(n - 1)
-        score(len(PLACE_CHUNKS) - 1)
+        def score_turned(n):
+            z_mx = quantise_z(n, z_words[n].bitcast(BF16), "z_codes%d" % n)
+            acc = bank(1 + n, [P, PACK, P])
+            for u in range(PACK):
+                product(acc[:, u, :], x_cand, planes[u], z_mx, True, True)
+            result = keep.tile([P, PACK, P], F32, name="result%d" % n)
+            nc.scalar.activation(result[:], acc[:], COPY, scale=0.0625)
+            nc.sync.dma_start(out_view[:, :, planes[n]], result[:])
+
+        right_turned(0, "fetched0", 7)
+        right_turned(1, "fetched1", 0)
+        rest = shared("rest", "fetched0", [P, PACK, P], F32)
+        for t in range(PACK):
+            nc.vector.scalar_tensor_tensor(rest[:, t, :], c_scaled[t][:, planes[last]], 4.0, e_scaled[t][:, planes[last]], ALU.mult, ALU.add)
+        right_turned(2, "rounded0", 7)
+
+        def right_direct(t):
+            nc.vector.tensor_tensor(z_last[:, planes[t]], e_scaled[t][:].indirect(entries(rt_list, P * last, S)), rest[:, t, :], ALU.subtract)
+
+        score_turned(0)
+        right_direct(0)
+        right_direct(1)
+        score_turned(1)
+        right_direct(2)
+        right_direct(3)
+        grouped = shared("z_grouped", "z_grouped", [P, PACK * P], BF16)
+        nc.vector.tensor_copy(
+            grouped[:].rearrange("p (c i t) -> p c t i", i=4, t=PACK),
+            z_last[:].rearrange("p (t c i) -> p c t i", i=4, t=PACK),
+        )
+        score_turned(2)
+        z_mx = quantise_z(last, grouped[:], "z_words2")
+        for h in range(2):
+            acc = bank(PACK * h, [P, 2, P])
+            for u in range(2):
+                product(acc[:, u, :], x_cand, planes[2 * h + u], z_mx, True, True)
+            result = keep.tile([P, 2, P], F32, name="last%d" % h)
+            nc.vector.tensor_scalar(result[:], acc[:], 0.0625, None, ALU.mult)
+            nc.sync.dma_start(out_view[:, 2 * h : 2 * h + 2, planes[last]], result[:])

@@ -3,7 +3,7 @@ from contextlib import ExitStack
 import concourse.mybir as mybir
 from concourse.masks import make_identity
 
-K, T, S, H, C = 512, 2048, 512, 512, 512
+K, T, S, H = 512, 2048, 512, 512
 FLOPS = 3 * 2 * K * H * S
 
 F32 = mybir.dt.float32
@@ -20,10 +20,14 @@ P = 128
 PACK = 4
 LANES = 16
 HALF = S // 2
-W_CHUNKS = ((0, 64), (64, 128))
-CHUNKS = S // P
-TURNED = 3
+OUT_SCALE = 0.0625
+
+W2_PARTS = ((0, 80), (80, 128))
+W1_PARTS = ((0, 48), (48, 96), (96, 128))
+
 SUMMED_PLANES = 3
+EARLY_GROUPS = 2
+TURNED = 3
 
 
 def tile_picked_fdtd8_none_p_kernel(tc, x_words, x_scales, w1, w2, gs, offs, two, lf, rt, cand, out):
@@ -32,61 +36,72 @@ def tile_picked_fdtd8_none_p_kernel(tc, x_words, x_scales, w1, w2, gs, offs, two
         keep = ctx.enter_context(tc.tile_pool(name="keep", bufs=1))
         psum = ctx.enter_context(tc.psum_pool(name="psum", bufs=1))
 
+        def sbuf(name, shape, dtype, reuses=None):
+            return keep.tile(shape, dtype, name=name, tag=reuses or name, align_bytes=64)
+
+        def bank(n, shape):
+            return psum.tile(shape, F32, name="bank%d" % n, tag="bank%d" % n)
+
         def load_list(name, src):
             tile = keep.tile([P, S // LANES], U16, name=name)
             nc.sync.dma_start(tile[:], src)
             return tile
 
-        def entries(tile, a, b):
-            return tile[:, a // LANES : b // LANES]
+        def entries(lists, a, b):
+            return lists[:, a // LANES : b // LANES]
 
-        def bank(n, shape):
-            return psum.tile(shape, F32, name="bank%d" % n, tag="bank%d" % n)
+        def block(n):
+            return slice(P * n, P * (n + 1))
 
-        table_scales = keep.tile([P, T], U8, name="table_scales", align_bytes=64)
+        table_scales = sbuf("table_scales", [P, T], U8)
         nc.vector.memset(table_scales[:].bitcast(I32), 0)
-        identity = keep.tile([P, P], F32, name="identity")
+        identity = sbuf("identity", [P, P], F32)
         make_identity(nc, identity[:])
         two_list = load_list("two_list", two)
         offs_list = load_list("offs_list", offs)
         cand_list = load_list("cand_list", cand)
         for q in range(4):
             nc.sync.dma_start(table_scales[32 * q : 32 * q + 4, :].bitcast(I32), x_scales[0][4 * q : 4 * q + 4, :].bitcast(I32))
-        table_words = keep.tile([P, T], U32, name="table_words", align_bytes=64)
-        nc.sync.dma_start(table_words[:].bitcast(I32), x_words[0].rearrange("p n t -> p (n t)").bitcast(I32))
 
-        def load_weight(name, w):
-            parts = []
-            for m0, m1 in W_CHUNKS:
-                part = keep.tile([P, PACK, PACK * (m1 - m0)], F32, name="%s_raw%d" % (name, m0), tag="%s_raw%d" % (name, m0))
-                nc.sync.dma_start(part[:], w.rearrange("(p j) c -> p j c", j=PACK)[:, :, PACK * m0 : PACK * m1])
-                parts.append(part)
-            return parts
+        def load_part(name, w, part):
+            m0, m1 = part
+            raw = sbuf("%s_raw%d" % (name, m0), [P, PACK, PACK * (m1 - m0)], F32)
+            nc.sync.dma_start(raw[:], w.rearrange("(p j) f -> p j f", j=PACK)[:, :, PACK * m0 : PACK * m1])
+            return raw
 
-        w2_raw = load_weight("w2", w2)
-        gain = keep.tile([P, PACK], F32, name="gain")
+        w2_raw = [load_part("w2", w2, W2_PARTS[0])]
+        table_words = sbuf("table_words", [P, T], U32)
+        nc.sync.dma_start(table_words[:].bitcast(I32), x_words[0].rearrange("p n j -> p (n j)").bitcast(I32))
+        w2_raw.append(load_part("w2", w2, W2_PARTS[1]))
+        w1_raw = [load_part("w1", w1, W1_PARTS[0])]
+        gain = sbuf("gain", [P, PACK], F32)
         nc.sync.dma_start(gain[:], gs.rearrange("(p t) o -> p (t o)", t=PACK))
-        w1_raw = load_weight("w1", w1)
+        w1_raw.extend(load_part("w1", w1, part) for part in W1_PARTS[1:])
         lf_list = load_list("lf_list", lf)
         rt_list = load_list("rt_list", rt)
+        w2_last_part = "w2_raw%d" % W2_PARTS[-1][0]
+        w1_last_part = "w1_raw%d" % W1_PARTS[-1][0]
 
-        def pick(name, table, dtype, lst, tag=None):
-            tile = keep.tile([P, S], dtype, name=name, tag=tag or name, align_bytes=64)
-            nc.vector.tensor_copy(tile[:], table[:].indirect(lst[:]))
-            return tile
+        def pick(name, table, dtype, lists, reuses=None):
+            picked = sbuf(name, [P, S], dtype, reuses)
+            nc.vector.tensor_copy(picked[:], table[:].indirect(lists[:]))
+            return picked
 
-        def deal(grouped, raw, m0, m1, scale):
-            nc.scalar.activation(
-                grouped[:].rearrange("p (t m j) -> p m j t", t=PACK, j=PACK)[:, m0:m1, :, :],
-                raw[:].rearrange("p j (m t) -> p m j t", t=PACK),
-                COPY,
-                scale=scale,
-            )
+        def deal(name, raws, parts, scale):
+            dealt = sbuf(name, [P, PACK * H], BF16)
+            for raw, (m0, m1) in zip(raws, parts):
+                nc.scalar.activation(
+                    dealt[:].rearrange("p (t m j) -> p m j t", t=PACK, j=PACK)[:, m0:m1, :, :],
+                    raw[:].rearrange("p j (m t) -> p m j t", t=PACK),
+                    COPY,
+                    scale=scale,
+                )
+            return dealt
 
-        def quantise(name, grouped, width):
-            codes = keep.tile([P, width], U32, name=name + "_codes", align_bytes=64)
-            scales = keep.tile([P, width], U8, name=name + "_scales", align_bytes=64)
-            nc.vector.quantize_mx(out=codes[:].bitcast(FP8X4), scales=scales[:], in_=grouped[:])
+        def quantise(name, values, width):
+            codes = sbuf(name + "_codes", [P, width], U32)
+            scales = sbuf(name + "_scales", [P, width], U8)
+            nc.vector.quantize_mx(out=codes[:].bitcast(FP8X4), scales=scales[:], in_=values)
             return codes, scales
 
         def product(dst, stationary, cols, moving, start, stop):
@@ -104,139 +119,138 @@ def tile_picked_fdtd8_none_p_kernel(tc, x_words, x_scales, w1, w2, gs, offs, two
         offs_scales = pick("offs_scales", table_scales, U8, offs_list)
         cand_scales = pick("cand_scales", table_scales, U8, cand_list)
 
-        w2_grouped = keep.tile([P, PACK * H], BF16, name="w2_grouped", tag="w2_grouped", align_bytes=64)
-        for (m0, m1), part in zip(W_CHUNKS, w2_raw):
-            deal(w2_grouped, part, m0, m1, 1.0)
-        w1_grouped = keep.tile([P, PACK * H], BF16, name="w1_grouped", tag="w1_grouped", align_bytes=64)
-        for (m0, m1), part in zip(W_CHUNKS, w1_raw):
-            deal(w1_grouped, part, m0, m1, 2.0)
-        factors = keep.tile([P, 3 * PACK], F32, name="factors", tag="w1_raw%d" % W_CHUNKS[-1][0])
-        factor, factor4, opposite = factors[:, :PACK], factors[:, PACK : 2 * PACK], factors[:, 2 * PACK :]
-        nc.scalar.activation(factor, gain[:], COPY, scale=-0.25)
+        w2_dealt = deal("w2_dealt", w2_raw, W2_PARTS, 1.0)
+        w1_dealt = deal("w1_dealt", w1_raw, W1_PARTS, 2.0)
+        factors = sbuf("factors", [P, 3 * PACK], F32)
+        g, g4, minus_g = factors[:, :PACK], factors[:, PACK : 2 * PACK], factors[:, 2 * PACK :]
+        nc.scalar.activation(g, gain[:], COPY, scale=-0.25)
 
         x_two = (pick("two_words", table_words, U32, two_list), two_scales)
         x_offs = (pick("offs_words", table_words, U32, offs_list), offs_scales)
-        w2_mx = quantise("w2", w2_grouped, H)
-        x_cand = (pick("cand_words", table_words, U32, cand_list, "w2_grouped"), cand_scales)
-        w1_mx = quantise("w1", w1_grouped, H)
+        w2_mx = quantise("w2", w2_dealt[:], H)
+        x_cand = (pick("cand_words", table_words, U32, cand_list, w2_last_part), cand_scales)
+        w1_mx = quantise("w1", w1_dealt[:], H)
 
-        planes = [slice(P * t, P * (t + 1)) for t in range(PACK)]
         c_banks = [bank(t, [P, S]) for t in range(PACK)]
         y_banks = [bank(PACK + t, [P, S]) for t in range(PACK)]
-        c_scaled = [keep.tile([P, S], F32, name="c_scaled%d" % t) for t in range(PACK)]
-        local = [keep.tile([P, S], F32, name="local%d" % t) for t in range(PACK)]
+        c_part = [sbuf("c_part%d" % t, [P, S], F32, w1_last_part if t == 0 else None) for t in range(PACK)]
+        c_left = sbuf("c_left", [P, S], F32)
+        local = {t: sbuf("local%d" % t, [P, S], F32) for t in range(1, PACK)}
+        c_pass, y_pass = (w2_mx, x_two), (w1_mx, x_offs)
         for t in range(PACK):
-            product(c_banks[t][:], w2_mx, planes[t], x_two, True, True)
-            nc.scalar.activation(c_scaled[t][:], c_banks[t][:], COPY, scale=factor[:, t : t + 1])
-            passes = [(w2_mx, x_two), (w1_mx, x_offs)]
-            if t == 2:
-                passes = passes[::-1]
-            if t == 3:
-                passes = passes[1:]
-            for u, (stationary, moving) in enumerate(passes):
-                product(y_banks[t][:], stationary, planes[t], moving, u == 0, u == len(passes) - 1)
-            if t == 0:
-                nc.scalar.activation(opposite, gain[:], COPY, scale=0.25)
+            product(c_banks[t][:], w2_mx, block(t), x_two, True, True)
+            nc.scalar.activation(c_part[t][:], c_banks[t][:], COPY, scale=g[:, t : t + 1])
+            if t < EARLY_GROUPS:
+                passes = [c_pass, y_pass]
             elif t < SUMMED_PLANES:
-                nc.scalar.activation(local[t][:], y_banks[t][:], COPY, scale=factor[:, t : t + 1])
-        nc.scalar.activation(factor4, gain[:], COPY, scale=-1.0)
+                passes = [y_pass, c_pass]
+            else:
+                passes = [y_pass]
+            for u, (stationary, moving) in enumerate(passes):
+                product(y_banks[t][:], stationary, block(t), moving, u == 0, u == len(passes) - 1)
+            if t == 0:
+                nc.scalar.activation(minus_g, gain[:], COPY, scale=0.25)
+            elif t < SUMMED_PLANES:
+                nc.scalar.activation(local[t][:], y_banks[t][:], COPY, scale=g[:, t : t + 1])
+        nc.scalar.activation(g4, gain[:], COPY, scale=-1.0)
 
-        turned = TURNED * P
-        c_full = []
+        c_part4 = []
         for t in range(PACK):
-            tile = keep.tile([P, turned], F32, name="c_full%d" % t)
-            nc.scalar.activation(tile[:], c_banks[t][:, :turned], COPY, scale=factor4[:, t : t + 1])
-            c_full.append(tile)
+            scaled = sbuf("c_part4_%d" % t, [P, TURNED * P], F32)
+            nc.scalar.activation(scaled[:], c_banks[t][:, : TURNED * P], COPY, scale=g4[:, t : t + 1])
+            c_part4.append(scaled)
 
         sums = [bank(PACK + n, [P, PACK, P]) for n in range(TURNED)]
 
         def add_turned(n, t, src, start, stop):
             nc.tensor.matmul(sums[n][:, t, :], src, identity[:], start=start, stop=stop, is_transpose=True)
 
-        e_scaled = [keep.tile([P, S], F32, name="e_scaled%d" % t) for t in range(PACK)]
+        halves = [slice(0, HALF), slice(HALF, S)]
+        e_part = [sbuf("e_part%d" % t, [P, S], F32) for t in range(PACK)]
         for t in range(PACK):
             if t == SUMMED_PLANES - 1:
-                nc.vector.scalar_tensor_tensor(local[t + 1][:], y_banks[t + 1][:], factor[:, t + 1 : t + 2], c_scaled[t + 1][:], ALU.mult, ALU.add)
-            for a in (0, HALF):
-                window = c_scaled[t][:].indirect(entries(lf_list, a, a + HALF))
-                if t == 0:
-                    nc.vector.tensor_copy(local[t][:, a : a + HALF], window)
-                else:
-                    nc.vector.tensor_tensor(e_scaled[t][:, a : a + HALF], window, local[t][:, a : a + HALF], ALU.subtract)
+                u = SUMMED_PLANES
+                nc.vector.scalar_tensor_tensor(local[u][:], y_banks[u][:], g[:, u : u + 1], c_part[u][:], ALU.mult, ALU.add)
             if t == 0:
-                nc.vector.scalar_tensor_tensor(e_scaled[t][:], y_banks[t][:], opposite[:, t : t + 1], local[t][:], ALU.mult, ALU.add)
+                for cols in halves:
+                    nc.vector.tensor_copy(c_left[:, cols], c_part[t][:].indirect(entries(lf_list, cols.start, cols.stop)))
+                for cols in halves:
+                    nc.vector.scalar_tensor_tensor(e_part[t][:, cols], y_banks[t][:, cols], minus_g[:, t : t + 1], c_left[:, cols], ALU.mult, ALU.add)
+            else:
+                for cols in halves:
+                    window = c_part[t][:].indirect(entries(lf_list, cols.start, cols.stop))
+                    nc.vector.tensor_tensor(e_part[t][:, cols], window, local[t][:, cols], ALU.subtract)
             for n in range(TURNED):
-                add_turned(n, t, c_full[t][:, planes[n]], t == 0, False)
-                add_turned(n, t, e_scaled[t][:, planes[n]], False, False)
+                add_turned(n, t, c_part4[t][:, block(n)], t == 0, False)
+                add_turned(n, t, e_part[t][:, block(n)], False, False)
 
-        out_view = out.rearrange("(a p) j -> p a j", p=P)
-        last = CHUNKS - 1
+        out_tiles = out.rearrange("(a p) j -> p a j", p=P)
+        last = TURNED
+        pairs = 2 * P
+        z_shared = sbuf("z_shared", [P, 3 * pairs], F32)
+        z_pairs = [z_shared[:, pairs : 2 * pairs], z_shared[:, 2 * pairs :], sbuf("z_pairs2", [P, pairs], F32)[:]]
 
-        def shared(name, tag, shape, dtype):
-            return keep.tile(shape, dtype, name=name, tag=tag, align_bytes=64)
-
-        z_last = shared("z_last", "z_last", [P, PACK * P], F32)
-        z_words = [z_last[:, 0:256], z_last[:, 256:512], shared("z_words2", "z_words2", [P, 2 * P], F32)[:]]
-
-        def right_turned(n, tag, back_bank):
-            fetched = shared("fetched%d" % n, tag, [P, PACK, P], F32)
+        def right_turned(first, count):
+            fetched = sbuf("fetched%d" % first, [P, PACK, count * P], F32)
             for t in range(PACK):
-                nc.vector.tensor_scalar(fetched[:, t, :], e_scaled[t][:].indirect(entries(rt_list, P * n, P * (n + 1))), -1.0, 0.0, ALU.mult, ALU.add)
-                add_turned(n, t, fetched[:, t, :], False, t == PACK - 1)
-            rounded = shared("rounded%d" % n, "rounded%d" % n, [P, PACK * P], BF16)
-            nc.scalar.activation(
-                rounded[:].rearrange("p (u m e) -> p u m e", u=2, e=2),
-                sums[n][:].rearrange("p (u e) m -> p u m e", e=2),
-                COPY,
-                scale=-1.0,
-            )
-            back = bank(back_bank, [P, 2, P])
+                window = e_part[t][:].indirect(entries(rt_list, P * first, P * (first + count)))
+                nc.vector.tensor_scalar(fetched[:, t, :], window, -1.0, 0.0, ALU.mult, ALU.add)
+                for n in range(count):
+                    add_turned(first + n, t, fetched[:, t, block(n)], False, t == PACK - 1)
+            tiles = []
+            for n in range(first, first + count):
+                rounded = sbuf("rounded%d" % n, [P, PACK * P], BF16)
+                nc.scalar.activation(
+                    rounded[:].rearrange("j (u p e) -> j u p e", u=2, e=2),
+                    sums[n][:].rearrange("j (u e) p -> j u p e", e=2),
+                    COPY,
+                    scale=-1.0,
+                )
+                tiles.append(rounded)
+            return tiles
+
+        def turn_back(n, rounded, bank_number):
+            back = bank(bank_number, [P, 2, P])
             for u in range(2):
-                nc.tensor.transpose(back[:, u, :], rounded[:].bitcast(F32)[:, planes[u]], identity[:])
-            nc.scalar.copy(z_words[n].rearrange("p (j u) -> p j u", u=2), back[:].rearrange("p u j -> p j u"))
+                nc.tensor.transpose(back[:, u, :], rounded[:].bitcast(F32)[:, block(u)], identity[:])
+            nc.scalar.copy(z_pairs[n].rearrange("p (j u) -> p j u", u=2), back[:].rearrange("p u j -> p j u"))
 
-        def quantise_z(n, grouped, tag):
-            codes = shared("z_codes%d" % n, tag, [P, P], U32)
-            scales = shared("z_scales%d" % n, "z_scales%d" % n, [P, P], U8)
-            nc.vector.quantize_mx(out=codes[:].bitcast(FP8X4), scales=scales[:], in_=grouped)
-            return codes, scales
+        def score(name, z, a, b, bank_numbers, final):
+            z_mx = quantise(name, z, b - a)
+            rows = PACK // len(bank_numbers)
+            for h, bank_number in enumerate(bank_numbers):
+                scores = bank(bank_number, [P, rows, b - a])
+                for u in range(rows):
+                    product(scores[:, u, :], x_cand, block(rows * h + u), z_mx, True, True)
+                result = sbuf("%s_result%d" % (name, h), [P, rows, b - a], F32)
+                if final and h == 1:
+                    nc.vector.tensor_scalar(result[:], scores[:], OUT_SCALE, None, ALU.mult)
+                else:
+                    nc.scalar.activation(result[:], scores[:], COPY, scale=OUT_SCALE)
+                queue = nc.scalar if final and h == 0 else nc.sync
+                queue.dma_start(out_tiles[:, rows * h : rows * (h + 1), a:b], result[:])
 
-        def score_turned(n):
-            z_mx = quantise_z(n, z_words[n].bitcast(BF16), "z_codes%d" % n)
-            acc = bank(1 + n, [P, PACK, P])
-            for u in range(PACK):
-                product(acc[:, u, :], x_cand, planes[u], z_mx, True, True)
-            result = keep.tile([P, PACK, P], F32, name="result%d" % n)
-            nc.scalar.activation(result[:], acc[:], COPY, scale=0.0625)
-            nc.sync.dma_start(out_view[:, :, planes[n]], result[:])
+        all_rounded = right_turned(0, 2) + right_turned(2, 1)
+        for n, bank_number in enumerate((7, 0, 1)):
+            turn_back(n, all_rounded[n], bank_number)
 
-        right_turned(0, "fetched0", 7)
-        right_turned(1, "fetched1", 0)
-        rest = shared("rest", "fetched0", [P, PACK, P], F32)
+        rest = sbuf("rest", [P, PACK, P], F32, "fetched0")
         for t in range(PACK):
-            nc.vector.scalar_tensor_tensor(rest[:, t, :], c_scaled[t][:, planes[last]], 4.0, e_scaled[t][:, planes[last]], ALU.mult, ALU.add)
-        right_turned(2, "rounded0", 7)
+            nc.vector.scalar_tensor_tensor(rest[:, t, :], c_part[t][:, block(last)], 4.0, e_part[t][:, block(last)], ALU.mult, ALU.add)
 
-        def right_direct(t):
-            nc.vector.tensor_tensor(z_last[:, planes[t]], e_scaled[t][:].indirect(entries(rt_list, P * last, S)), rest[:, t, :], ALU.subtract)
+        def right_last(t):
+            window = e_part[t][:].indirect(entries(rt_list, P * last, S))
+            nc.vector.tensor_tensor(z_shared[:, block(t)], window, rest[:, t, :], ALU.subtract)
 
-        score_turned(0)
-        right_direct(0)
-        right_direct(1)
-        score_turned(1)
-        right_direct(2)
-        right_direct(3)
-        grouped = shared("z_grouped", "z_grouped", [P, PACK * P], BF16)
+        right_last(0)
+        right_last(1)
+        score("z01", z_shared[:, pairs:].bitcast(BF16), 0, 2 * P, (2, 3), False)
+        score("z2", z_pairs[2].bitcast(BF16), 2 * P, 3 * P, (4,), False)
+        right_last(2)
+        right_last(3)
+        z_last = sbuf("z_last", [P, PACK * P], BF16)
         nc.vector.tensor_copy(
-            grouped[:].rearrange("p (c i t) -> p c t i", i=4, t=PACK),
-            z_last[:].rearrange("p (t c i) -> p c t i", i=4, t=PACK),
+            z_last[:].rearrange("p (c i t) -> p c t i", i=4, t=PACK),
+            z_shared[:, : PACK * P].rearrange("p (t c i) -> p c t i", i=4, t=PACK),
         )
-        score_turned(2)
-        z_mx = quantise_z(last, grouped[:], "z_words2")
-        for h in range(2):
-            acc = bank(PACK * h, [P, 2, P])
-            for u in range(2):
-                product(acc[:, u, :], x_cand, planes[2 * h + u], z_mx, True, True)
-            result = keep.tile([P, 2, P], F32, name="last%d" % h)
-            nc.vector.tensor_scalar(result[:], acc[:], 0.0625, None, ALU.mult)
-            nc.sync.dma_start(out_view[:, 2 * h : 2 * h + 2, planes[last]], result[:])
+        score("z3", z_last[:], P * last, S, (5, 6), True)

from contextlib import ExitStack

import concourse.mybir as mybir
from concourse.masks import make_identity

K, T, S, H = 512, 2048, 512, 512
FLOPS = 3 * 2 * K * H * S

F32 = mybir.dt.float32
BF16 = mybir.dt.bfloat16
I32 = mybir.dt.int32
U32 = mybir.dt.uint32
U16 = mybir.dt.uint16
U8 = mybir.dt.uint8
FP8X4 = mybir.dt.float8_e4m3fn_x4
ALU = mybir.AluOpType
COPY = mybir.ActivationFunctionType.Copy

P = 128
PACK = 4
LANES = 16
HALF = S // 2
OUT_SCALE = 0.0625

W2_PARTS = ((0, 80), (80, 128))
W1_PARTS = ((0, 48), (48, 96), (96, 128))

SUMMED_PLANES = 3
EARLY_GROUPS = 2
TURNED = 3


def tile_picked_fdtd8_none_p_kernel(tc, x_words, x_scales, w1, w2, gs, offs, two, lf, rt, cand, out):
    nc = tc.nc
    with ExitStack() as ctx:
        keep = ctx.enter_context(tc.tile_pool(name="keep", bufs=1))
        psum = ctx.enter_context(tc.psum_pool(name="psum", bufs=1))

        def sbuf(name, shape, dtype, reuses=None):
            return keep.tile(shape, dtype, name=name, tag=reuses or name, align_bytes=64)

        def bank(n, shape):
            return psum.tile(shape, F32, name="bank%d" % n, tag="bank%d" % n)

        def load_list(name, src):
            tile = keep.tile([P, S // LANES], U16, name=name)
            nc.sync.dma_start(tile[:], src)
            return tile

        def entries(lists, a, b):
            return lists[:, a // LANES : b // LANES]

        def block(n):
            return slice(P * n, P * (n + 1))

        table_scales = sbuf("table_scales", [P, T], U8)
        nc.vector.memset(table_scales[:].bitcast(I32), 0)
        identity = sbuf("identity", [P, P], F32)
        make_identity(nc, identity[:])
        two_list = load_list("two_list", two)
        offs_list = load_list("offs_list", offs)
        cand_list = load_list("cand_list", cand)
        for q in range(4):
            nc.sync.dma_start(table_scales[32 * q : 32 * q + 4, :].bitcast(I32), x_scales[0][4 * q : 4 * q + 4, :].bitcast(I32))

        def load_part(name, w, part):
            m0, m1 = part
            raw = sbuf("%s_raw%d" % (name, m0), [P, PACK, PACK * (m1 - m0)], F32)
            nc.sync.dma_start(raw[:], w.rearrange("(p j) f -> p j f", j=PACK)[:, :, PACK * m0 : PACK * m1])
            return raw

        w2_raw = [load_part("w2", w2, W2_PARTS[0])]
        table_words = sbuf("table_words", [P, T], U32)
        nc.sync.dma_start(table_words[:].bitcast(I32), x_words[0].rearrange("p n j -> p (n j)").bitcast(I32))
        w2_raw.append(load_part("w2", w2, W2_PARTS[1]))
        w1_raw = [load_part("w1", w1, W1_PARTS[0])]
        gain = sbuf("gain", [P, PACK], F32)
        nc.sync.dma_start(gain[:], gs.rearrange("(p t) o -> p (t o)", t=PACK))
        w1_raw.extend(load_part("w1", w1, part) for part in W1_PARTS[1:])
        lf_list = load_list("lf_list", lf)
        rt_list = load_list("rt_list", rt)
        w2_last_part = "w2_raw%d" % W2_PARTS[-1][0]
        w1_last_part = "w1_raw%d" % W1_PARTS[-1][0]

        def pick(name, table, dtype, lists, reuses=None):
            picked = sbuf(name, [P, S], dtype, reuses)
            nc.vector.tensor_copy(picked[:], table[:].indirect(lists[:]))
            return picked

        def deal(name, raws, parts, scale):
            dealt = sbuf(name, [P, PACK * H], BF16)
            for raw, (m0, m1) in zip(raws, parts):
                nc.scalar.activation(
                    dealt[:].rearrange("p (t m j) -> p m j t", t=PACK, j=PACK)[:, m0:m1, :, :],
                    raw[:].rearrange("p j (m t) -> p m j t", t=PACK),
                    COPY,
                    scale=scale,
                )
            return dealt

        def quantise(name, values, width):
            codes = sbuf(name + "_codes", [P, width], U32)
            scales = sbuf(name + "_scales", [P, width], U8)
            nc.vector.quantize_mx(out=codes[:].bitcast(FP8X4), scales=scales[:], in_=values)
            return codes, scales

        def product(dst, stationary, cols, moving, start, stop):
            nc.tensor.matmul_mx(
                out=dst,
                lhsT=stationary[0][:, cols].bitcast(FP8X4),
                lhsT_scale=stationary[1][:, cols],
                rhs=moving[0][:].bitcast(FP8X4),
                rhs_scale=moving[1][:],
                start=start,
                stop=stop,
            )

        two_scales = pick("two_scales", table_scales, U8, two_list)
        offs_scales = pick("offs_scales", table_scales, U8, offs_list)
        cand_scales = pick("cand_scales", table_scales, U8, cand_list)

        w2_dealt = deal("w2_dealt", w2_raw, W2_PARTS, 1.0)
        w1_dealt = deal("w1_dealt", w1_raw, W1_PARTS, 2.0)
        factors = sbuf("factors", [P, 3 * PACK], F32)
        g, g4, minus_g = factors[:, :PACK], factors[:, PACK : 2 * PACK], factors[:, 2 * PACK :]
        nc.scalar.activation(g, gain[:], COPY, scale=-0.25)

        x_two = (pick("two_words", table_words, U32, two_list), two_scales)
        x_offs = (pick("offs_words", table_words, U32, offs_list), offs_scales)
        w2_mx = quantise("w2", w2_dealt[:], H)
        x_cand = (pick("cand_words", table_words, U32, cand_list, w2_last_part), cand_scales)
        w1_mx = quantise("w1", w1_dealt[:], H)

        c_banks = [bank(t, [P, S]) for t in range(PACK)]
        y_banks = [bank(PACK + t, [P, S]) for t in range(PACK)]
        c_part = [sbuf("c_part%d" % t, [P, S], F32, w1_last_part if t == 0 else None) for t in range(PACK)]
        c_left = sbuf("c_left", [P, S], F32)
        local = {t: sbuf("local%d" % t, [P, S], F32) for t in range(1, PACK)}
        c_pass, y_pass = (w2_mx, x_two), (w1_mx, x_offs)
        for t in range(PACK):
            product(c_banks[t][:], w2_mx, block(t), x_two, True, True)
            nc.scalar.activation(c_part[t][:], c_banks[t][:], COPY, scale=g[:, t : t + 1])
            if t < EARLY_GROUPS:
                passes = [c_pass, y_pass]
            elif t < SUMMED_PLANES:
                passes = [y_pass, c_pass]
            else:
                passes = [y_pass]
            for u, (stationary, moving) in enumerate(passes):
                product(y_banks[t][:], stationary, block(t), moving, u == 0, u == len(passes) - 1)
            if t == 0:
                nc.scalar.activation(minus_g, gain[:], COPY, scale=0.25)
            elif t < SUMMED_PLANES:
                nc.scalar.activation(local[t][:], y_banks[t][:], COPY, scale=g[:, t : t + 1])
        nc.scalar.activation(g4, gain[:], COPY, scale=-1.0)

        c_part4 = []
        for t in range(PACK):
            scaled = sbuf("c_part4_%d" % t, [P, TURNED * P], F32)
            nc.scalar.activation(scaled[:], c_banks[t][:, : TURNED * P], COPY, scale=g4[:, t : t + 1])
            c_part4.append(scaled)

        sums = [bank(PACK + n, [P, PACK, P]) for n in range(TURNED)]

        def add_turned(n, t, src, start, stop):
            nc.tensor.matmul(sums[n][:, t, :], src, identity[:], start=start, stop=stop, is_transpose=True)

        halves = [slice(0, HALF), slice(HALF, S)]
        e_part = [sbuf("e_part%d" % t, [P, S], F32) for t in range(PACK)]
        for t in range(PACK):
            if t == SUMMED_PLANES - 1:
                u = SUMMED_PLANES
                nc.vector.scalar_tensor_tensor(local[u][:], y_banks[u][:], g[:, u : u + 1], c_part[u][:], ALU.mult, ALU.add)
            if t == 0:
                for cols in halves:
                    nc.vector.tensor_copy(c_left[:, cols], c_part[t][:].indirect(entries(lf_list, cols.start, cols.stop)))
                for cols in halves:
                    nc.vector.scalar_tensor_tensor(e_part[t][:, cols], y_banks[t][:, cols], minus_g[:, t : t + 1], c_left[:, cols], ALU.mult, ALU.add)
            else:
                for cols in halves:
                    window = c_part[t][:].indirect(entries(lf_list, cols.start, cols.stop))
                    nc.vector.tensor_tensor(e_part[t][:, cols], window, local[t][:, cols], ALU.subtract)
            for n in range(TURNED):
                add_turned(n, t, c_part4[t][:, block(n)], t == 0, False)
                add_turned(n, t, e_part[t][:, block(n)], False, False)

        out_tiles = out.rearrange("(a p) j -> p a j", p=P)
        last = TURNED
        pairs = 2 * P
        z_shared = sbuf("z_shared", [P, 3 * pairs], F32)
        z_pairs = [z_shared[:, pairs : 2 * pairs], z_shared[:, 2 * pairs :], sbuf("z_pairs2", [P, pairs], F32)[:]]

        def right_turned(first, count):
            fetched = sbuf("fetched%d" % first, [P, PACK, count * P], F32)
            for t in range(PACK):
                window = e_part[t][:].indirect(entries(rt_list, P * first, P * (first + count)))
                nc.vector.tensor_scalar(fetched[:, t, :], window, -1.0, 0.0, ALU.mult, ALU.add)
                for n in range(count):
                    add_turned(first + n, t, fetched[:, t, block(n)], False, t == PACK - 1)
            tiles = []
            for n in range(first, first + count):
                rounded = sbuf("rounded%d" % n, [P, PACK * P], BF16)
                nc.scalar.activation(
                    rounded[:].rearrange("j (u p e) -> j u p e", u=2, e=2),
                    sums[n][:].rearrange("j (u e) p -> j u p e", e=2),
                    COPY,
                    scale=-1.0,
                )
                tiles.append(rounded)
            return tiles

        def turn_back(n, rounded, bank_number):
            back = bank(bank_number, [P, 2, P])
            for u in range(2):
                nc.tensor.transpose(back[:, u, :], rounded[:].bitcast(F32)[:, block(u)], identity[:])
            nc.scalar.copy(z_pairs[n].rearrange("p (j u) -> p j u", u=2), back[:].rearrange("p u j -> p j u"))

        def score(name, z, a, b, bank_numbers, final):
            z_mx = quantise(name, z, b - a)
            rows = PACK // len(bank_numbers)
            for h, bank_number in enumerate(bank_numbers):
                scores = bank(bank_number, [P, rows, b - a])
                for u in range(rows):
                    product(scores[:, u, :], x_cand, block(rows * h + u), z_mx, True, True)
                result = sbuf("%s_result%d" % (name, h), [P, rows, b - a], F32)
                if final and h == 1:
                    nc.vector.tensor_scalar(result[:], scores[:], OUT_SCALE, None, ALU.mult)
                else:
                    nc.scalar.activation(result[:], scores[:], COPY, scale=OUT_SCALE)
                queue = nc.scalar if final and h == 0 else nc.sync
                queue.dma_start(out_tiles[:, rows * h : rows * (h + 1), a:b], result[:])

        all_rounded = right_turned(0, 2) + right_turned(2, 1)
        for n, bank_number in enumerate((7, 0, 1)):
            turn_back(n, all_rounded[n], bank_number)

        rest = sbuf("rest", [P, PACK, P], F32, "fetched0")
        for t in range(PACK):
            nc.vector.scalar_tensor_tensor(rest[:, t, :], c_part[t][:, block(last)], 4.0, e_part[t][:, block(last)], ALU.mult, ALU.add)

        def right_last(t):
            window = e_part[t][:].indirect(entries(rt_list, P * last, S))
            nc.vector.tensor_tensor(z_shared[:, block(t)], window, rest[:, t, :], ALU.subtract)

        right_last(0)
        right_last(1)
        score("z01", z_shared[:, pairs:].bitcast(BF16), 0, 2 * P, (2, 3), False)
        score("z2", z_pairs[2].bitcast(BF16), 2 * P, 3 * P, (4,), False)
        right_last(2)
        right_last(3)
        z_last = sbuf("z_last", [P, PACK * P], BF16)
        nc.vector.tensor_copy(
            z_last[:].rearrange("p (c i t) -> p c t i", i=4, t=PACK),
            z_shared[:, : PACK * P].rearrange("p (t c i) -> p c t i", i=4, t=PACK),
        )
        score("z3", z_last[:], P * last, S, (5, 6), True)
